import numpy as np
import ml_dtypes


def mxq(x, axis, fmt="e4m3"):
    dtype, down = {"e4m3": (ml_dtypes.float8_e4m3fn, 7), "e5m2": (ml_dtypes.float8_e5m2, 14)}[fmt]
    v = np.moveaxis(np.asarray(x, np.float32).astype(ml_dtypes.bfloat16).astype(np.float64), axis, -1)
    blocks = v.reshape(v.shape[:-1] + (-1, 32))
    amax = np.abs(blocks).max(-1, keepdims=True)
    byte = np.maximum(np.where(amax > 0, np.frexp(amax)[1] - 1 + 127, 0) - down, 1)
    scale = np.exp2(byte - 127.0)
    codes = (blocks / scale).astype(np.float32).astype(dtype).astype(np.float64)
    return np.moveaxis((codes * scale).reshape(v.shape), -1, axis)


WIDE = False


def mx_kscale(k):
    if not WIDE:
        return np.ones(k)
    levels = np.array([10, -10, 5, -5, 0])
    if k % 512:
        return np.exp2(np.random.permutation(np.resize(levels, k // 32))).repeat(32)
    a = np.empty((k // 512, 16))
    for p in range(k // 512):
        a[p, :8] = np.random.permutation(np.resize(levels, 8))
        for g in range(8):
            far = levels[np.abs(levels - a[p, g]) >= 10]
            a[p, g + 8] = far[np.random.randint(len(far))]
    return np.exp2(a.ravel()).repeat(32)


def f64(x):
    return np.asarray(x).astype(np.float64)


def striped(idx):
    return np.tile(idx.reshape(-1, 16).T, (8, 1)).astype(np.uint16)


def unstriped(offs):
    return offs[:16].T.reshape(-1).astype(np.int64)


E2M1 = np.array([0.0, 0.5, 1.0, 1.5, 2.0, 3.0, 4.0, 6.0, -0.0, -0.5, -1.0, -1.5, -2.0, -3.0, -4.0, -6.0])


def pack_weight(w, fmt):
    k, n = w.shape
    w = f64(np.asarray(w, np.float32).astype(ml_dtypes.bfloat16)).reshape(k // 32, 32, n)
    amax = np.abs(w).max(1)
    if fmt == "e4m3":
        byte = np.frexp(amax)[1] - 1 + 127 - 7
    else:
        mant, ex = np.frexp(amax / 6.0)
        byte = np.where(mant > 0.5, ex, ex - 1) + 127
    byte = np.clip(np.where(amax > 0, byte, 1), 1, 254)
    scaled = (w * np.exp2(127.0 - byte)[:, None, :]).reshape(k, n).astype(np.float32)
    by_word = np.ascontiguousarray(scaled.reshape(k // 512, 128, 4, n).transpose(0, 1, 3, 2))
    if fmt == "e4m3":
        words = by_word.astype(ml_dtypes.float8_e4m3fn).view(np.uint8)
    else:
        c = by_word.astype(ml_dtypes.float4_e2m1fn).view(np.uint8) & 0xF
        words = (c[..., 0::2] | (c[..., 1::2] << 4)).reshape(k // 512, 128, 2 * n)
    return np.ascontiguousarray(words), np.ascontiguousarray(byte.astype(np.uint8).reshape(k // 512, 16, n))


def unpack_weight(words, scales, fmt):
    g, _, n = scales.shape
    words = np.ascontiguousarray(words).reshape(g, 128, n, -1)
    if fmt == "e4m3":
        vals = words.view(ml_dtypes.float8_e4m3fn).astype(np.float64)
    else:
        nib = np.empty((g, 128, n, 4), np.uint8)
        nib[..., 0::2] = words & 0xF
        nib[..., 1::2] = words >> 4
        vals = E2M1[nib]
    vals = vals * np.repeat(np.exp2(scales.astype(np.float64) - 127.0), 8, axis=1)[..., None]
    return vals.transpose(0, 1, 3, 2).reshape(g * 512, n)


def gelu(v):
    return 0.5 * v * (1.0 + np.tanh(np.sqrt(2.0 / np.pi) * (v + 0.044715 * v**3)))


def striped8(idx):
    return np.concatenate([v.reshape(-1, 16).T for v in idx]).astype(np.uint16)


def unstriped8(offs):
    return np.stack([offs[16 * g:16 * g + 16].T.reshape(-1) for g in range(8)]).astype(np.int64)


def runs(v, idx8):
    k = np.arange(v.shape[0])
    return v[k[:, None], idx8[k % 512 // 64]]


K, T, S, H, P, N = 1024, 2048, 1024, 1024, 512, 512


def setup_inputs():
    n = np.random.standard_normal
    s = mx_kscale(K)[:, None]
    u = mx_kscale(H)[:, None]
    d = {}
    d["tab_words"], d["tab_scales"] = pack_weight(n((K, T)) * s, "e4m3")
    d["offs"] = striped8(np.stack([np.random.permutation(T)[:S] for _ in range(8)]))
    d["w1"] = (n((K, H)) / K**0.5 / s).astype(np.float32)
    d["w4_words"], d["w4_scales"] = pack_weight(n((K, H)) / K**0.5 / s, "e2m1")
    d["gain"] = (np.exp(0.3 * n(H)) * u[:, 0]).astype(np.float32)
    d["pos1"] = striped(np.random.permutation(S)[:P])
    d["pos2"] = striped(np.random.permutation(S)[:P])
    d["w8_words"], d["w8_scales"] = pack_weight(1.4 * n((H, N)) / H**0.5 / u, "e4m3")
    return d


def reference(tab_words, tab_scales, offs, w1, w4_words, w4_scales, gain, pos1, pos2, w8_words, w8_scales):
    v = runs(unpack_weight(tab_words, tab_scales, "e4m3"), unstriped8(offs))
    a = mxq(f64(w1), 0, "e4m3").T @ v
    b = unpack_weight(w4_words, w4_scales, "e2m1").T @ v
    h = (a * b + a + b) * f64(gain)[:, None]
    push = h[:, unstriped(pos1)]
    draw = h[:, unstriped(pos2)]
    z = np.maximum(push, np.abs(draw))
    y = unpack_weight(w8_words, w8_scales, "e4m3").T @ mxq(z, 0, "e4m3")
    return 1.0 / (1.0 + np.exp(-y))

@@ -1,0 +1,272 @@
+from contextlib import ExitStack
+
+import concourse.mybir as mybir
+
+K, T, S, H, PAIRS, N = 1024, 2048, 1024, 1024, 512, 512
+FLOPS = 2 * (2 * K * H * S + H * N * PAIRS)
+
+F32 = mybir.dt.float32
+BF16 = mybir.dt.bfloat16
+I32 = mybir.dt.int32
+U32 = mybir.dt.uint32
+U16 = mybir.dt.uint16
+U8 = mybir.dt.uint8
+FP8X4 = mybir.dt.float8_e4m3fn_x4
+FP4X4 = mybir.dt.float4_e2m1fn_x4
+ALU = mybir.AluOpType
+ACT = mybir.ActivationFunctionType
+
+P = 128
+PACK = 4
+PASS = P * PACK
+BANK = 512
+QUARTER = 128
+
+
+def tile_list_reed_voicing_scores_kernel(
+    tc, tab_words, tab_scales, offs, w1, w4_words, w4_scales, gain, pos1, pos2, w8_words, w8_scales, out
+):
+    nc = tc.nc
+    with ExitStack() as ctx:
+        keep = ctx.enter_context(tc.tile_pool(name="keep", bufs=1))
+        ring = ctx.enter_context(tc.tile_pool(name="ring", bufs=2))
+        psum = ctx.enter_context(tc.psum_pool(name="psum", bufs=8))
+
+        def held(shape, dtype, name):
+            return keep.tile(shape, dtype, name=name, align_bytes=64)
+
+        offs_t = keep.tile([P, S // 16], U16, name="offs_t")
+        pos1_t = keep.tile([P, PAIRS // 16], U16, name="pos1_t")
+        pos2_t = keep.tile([P, PAIRS // 16], U16, name="pos2_t")
+        tab_sc = [held([P, T], U8, "tab_sc%d" % a) for a in range(2)]
+        tab_w = [held([P, T], U32, "tab_w%d" % a) for a in range(2)]
+        picked_sc = held([P, 2 * S], U8, "picked_sc")
+        v_sc = held([P, 2 * S], U8, "v_sc")
+        v_w = [held([P, S], U32, "v_w%d" % a) for a in range(2)]
+        w4_sc_raw = held([P, 2, H], U8, "w4_sc_raw")
+        w8_sc = held([P, 2, N], U8, "w8_sc")
+        gain_t = held([P, 2, PACK], F32, "gain_t")
+
+        for a in range(2):
+            nc.vector.memset(tab_sc[a][:].bitcast(I32), 0)
+        nc.gpsimd.memset(w4_sc_raw[:].rearrange("p a c -> p (a c)").bitcast(I32), 0)
+        nc.vector.memset(w8_sc[:].rearrange("p a c -> p (a c)").bitcast(I32), 0)
+        nc.vector.memset(v_sc[:].bitcast(I32), 0)
+
+        def load_w1(b, a):
+            raw = ring.tile([P, PACK, PASS], F32, name="w1_raw", bufs=2)
+            rows = w1[PASS * a : PASS * (a + 1), PASS * b : PASS * (b + 1)]
+            nc.sync.dma_start(out=raw[:], in_=rows.rearrange("(p j) c -> p j c", j=PACK))
+            return raw
+
+        def load_w4(b):
+            raw = held([P, 2, PASS], U16, "w4_raw")
+            cols = w4_words[:, :, 2 * PASS * b : 2 * PASS * (b + 1)]
+            nc.sync.dma_start(out=raw[:].bitcast(I32), in_=cols.rearrange("a p c -> p a c").bitcast(I32))
+            return raw
+
+        def load_tab(a):
+            nc.sync.dma_start(
+                out=tab_w[a][:].bitcast(I32), in_=tab_words[a].rearrange("p t i -> p (t i)").bitcast(I32)
+            )
+
+        nc.sync.dma_start(offs_t[:], offs)
+        nc.sync.dma_start(pos1_t[:], pos1)
+        nc.sync.dma_start(pos2_t[:], pos2)
+        for a in range(2):
+            nc.sync.dma_start(out=tab_sc[a][0:P:8, :].bitcast(I32), in_=tab_scales[a].bitcast(I32))
+        load_tab(0)
+        w1_raw = {(0, a): load_w1(0, a) for a in range(2)}
+        w4_raw = [load_w4(0)]
+        load_tab(1)
+        for r in range(4):
+            nc.gpsimd.dma_start(
+                out=w4_sc_raw[r:P:32].bitcast(I32),
+                in_=w4_scales[:, r:16:4, :].rearrange("a q c -> q a c").bitcast(I32),
+            )
+        nc.gpsimd.dma_start(out=gain_t[:], in_=gain.rearrange("(b p t) -> p b t", b=2, t=PACK))
+        for r in range(4):
+            nc.gpsimd.dma_start(
+                out=w8_sc[r:P:32].bitcast(I32),
+                in_=w8_scales[:, r:16:4, :].rearrange("a q c -> q a c").bitcast(I32),
+            )
+
+        for a in range(2):
+            nc.vector.tensor_copy(picked_sc[:, S * a : S * (a + 1)], tab_sc[a][:].indirect(offs_t[:]))
+        for r in range(4):
+            nc.sync.dma_start(out=v_sc[r:P:32, :].bitcast(I32), in_=picked_sc[8 * r : P : 32, :].bitcast(I32))
+        nc.vector.tensor_copy(v_w[0][:], tab_w[0][:].indirect(offs_t[:]))
+
+        def round_w1(b, a):
+            grouped = ring.tile([P, PACK * PASS], BF16, name="w1_bf", bufs=2, align_bytes=64)
+            nc.scalar.copy(
+                out=grouped[:].rearrange("p (t m j) -> p m j t", t=PACK, j=PACK),
+                in_=w1_raw[b, a][:].rearrange("p j (m t) -> p m j t", t=PACK),
+            )
+            return grouped
+
+        def quantize_w1(b, a, grouped):
+            codes = held([P, PASS], U32, "w1_codes%d%d" % (b, a))
+            scales = held([P, PASS], U8, "w1_scales%d%d" % (b, a))
+            nc.vector.quantize_mx(out=codes[:].bitcast(FP8X4), scales=scales[:], in_=grouped[:])
+            return codes, scales
+
+        def deal_w4(b):
+            words = held([P, 2, PASS], U16, "w4_w%d" % b)
+            scales = held([P, 2, PASS], U8, "w4_sc%d" % b)
+            nc.vector.tensor_copy(
+                out=scales[:].rearrange("p a (t m) -> p a t m", t=PACK),
+                in_=w4_sc_raw[:, :, PASS * b : PASS * (b + 1)].rearrange("p a (m t) -> p a t m", t=PACK),
+            )
+            nc.vector.tensor_copy(
+                out=words[:].rearrange("p a (t m) -> p a t m", t=PACK),
+                in_=w4_raw[b][:].rearrange("p a (m t) -> p a t m", t=PACK),
+            )
+            return words, scales
+
+        def gather_words(half):
+            nc.vector.tensor_copy(
+                v_w[1][:, BANK * half : BANK * (half + 1)],
+                tab_w[1][:].indirect(offs_t[:, 32 * half : 32 * (half + 1)]),
+            )
+
+        w1_q = {}
+        w1_bf = {(0, a): round_w1(0, a) for a in range(2)}
+        w1_q[0, 0] = quantize_w1(0, 0, w1_bf[0, 0])
+        w4_q = [deal_w4(0)]
+        gather_words(0)
+        w1_q[0, 1] = quantize_w1(0, 1, w1_bf[0, 1])
+        gather_words(1)
+
+        for a in range(2):
+            w1_raw[1, a] = load_w1(1, a)
+        w4_raw.append(load_w4(1))
+        w8_w = held([P, 2, N], U32, "tab_w1")
+        nc.sync.dma_start(
+            out=w8_w[:].bitcast(I32), in_=w8_words.rearrange("a p c i -> p a (c i)").bitcast(I32)
+        )
+
+        def first_stage(b, t):
+            rows = slice(P * t, P * (t + 1))
+            g = gain_t[:, b, t : t + 1]
+            gb = ring.tile([P, S], F32, name="gb", bufs=3)
+            prod = ring.tile([P, S], F32, name="prod", bufs=2)
+            for half in range(2):
+                cols = slice(BANK * half, BANK * (half + 1))
+                b_acc = psum.tile([P, BANK], F32, name="acc")
+                a_acc = psum.tile([P, BANK], F32, name="acc")
+                for a in range(2):
+                    nc.tensor.matmul_mx(
+                        out=b_acc[:],
+                        lhsT=w4_q[b][0][:, a, rows].bitcast(FP4X4),
+                        lhsT_scale=w4_q[b][1][:, a, rows],
+                        rhs=v_w[a][:, cols].bitcast(FP8X4),
+                        rhs_scale=v_sc[:, S * a + BANK * half : S * a + BANK * (half + 1)],
+                        start=(a == 0),
+                        stop=(a == 1),
+                    )
+                for a in range(2):
+                    nc.tensor.matmul_mx(
+                        out=a_acc[:],
+                        lhsT=w1_q[b, a][0][:, rows].bitcast(FP8X4),
+                        lhsT_scale=w1_q[b, a][1][:, rows],
+                        rhs=v_w[a][:, cols].bitcast(FP8X4),
+                        rhs_scale=v_sc[:, S * a + BANK * half : S * a + BANK * (half + 1)],
+                        start=(a == 0),
+                        stop=(a == 1),
+                    )
+                nc.scalar.activation(out=gb[:, cols], in_=b_acc[:], func=ACT.Copy, scale=g)
+                nc.vector.scalar_tensor_tensor(
+                    out=prod[:, cols], in0=gb[:, cols], scalar=g, in1=a_acc[:], op0=ALU.add, op1=ALU.mult
+                )
+            return gb, prod
+
+        def join(gb, prod):
+            h = ring.tile([P, S], F32, name="h", bufs=3)
+            nc.vector.tensor_tensor(out=h[:], in0=prod[:], in1=gb[:], op=ALU.add)
+            return h
+
+        push = [held([P, PACK, PAIRS], F32, "push%d" % b) for b in range(2)]
+        size = [held([P, PACK, PAIRS], F32, "size%d" % b) for b in range(2)]
+
+        def fetch_draw(b, t, h):
+            draw = ring.tile([P, PAIRS], F32, name="draw", bufs=2)
+            nc.vector.tensor_copy(draw[:], h[:].indirect(pos2_t[:]))
+            nc.scalar.activation(out=size[b][:, t, :], in_=draw[:], func=ACT.Abs)
+
+        def fetch_push(b, t, h):
+            nc.vector.tensor_copy(push[b][:, t, :], h[:].indirect(pos1_t[:]))
+
+        def make_z(b, q):
+            cols = slice(QUARTER * q, QUARTER * (q + 1))
+            z = ring.tile([P, PACK * QUARTER], BF16, name="z", bufs=4, align_bytes=64)
+            nc.vector.tensor_tensor(
+                out=z[:].rearrange("p (c i t) -> p c t i", i=4, t=PACK),
+                in0=push[b][:, :, cols].rearrange("p t (c i) -> p c t i", i=4),
+                in1=size[b][:, :, cols].rearrange("p t (c i) -> p c t i", i=4),
+                op=ALU.max,
+            )
+            return z
+
+        def quantize_z(b, q, z):
+            codes = held([P, QUARTER], U32, "z_codes%d%d" % (b, q))
+            scales = held([P, QUARTER], U8, "z_scales%d%d" % (b, q))
+            nc.vector.quantize_mx(out=codes[:].bitcast(FP8X4), scales=scales[:], in_=z[:])
+            return codes, scales
+
+        def second_pass(b, y, z_q):
+            for n in range(4):
+                cols = slice(P * n, P * (n + 1))
+                nc.tensor.matmul_mx(
+                    out=y[:, cols],
+                    lhsT=w8_w[:, b, cols].bitcast(FP8X4),
+                    lhsT_scale=w8_sc[:, b, cols],
+                    rhs=z_q[0][:].bitcast(FP8X4),
+                    rhs_scale=z_q[1][:],
+                    start=(b == 0 and n == 0),
+                    stop=(b == 1 and n == 3),
+                )
+
+        def finish_block(b, after):
+            z = [make_z(b, 0)]
+            for q in range(4):
+                if q < 3:
+                    z.append(make_z(b, q + 1))
+                after(q, quantize_z(b, q, z[q]))
+
+        slices = [(b, t) for b in range(2) for t in range(PACK)]
+        z_q0 = []
+        h_prev = None
+        for s, (b, t) in enumerate(slices):
+            gb, prod = first_stage(b, t)
+            if s > 0:
+                fetch_draw(*slices[s - 1], h_prev)
+            h = join(gb, prod)
+            if s > 0:
+                fetch_push(*slices[s - 1], h_prev)
+            h_prev = h
+            if s in (1, 2):
+                w1_bf[1, s - 1] = round_w1(1, s - 1)
+                w1_q[1, s - 1] = quantize_w1(1, s - 1, w1_bf[1, s - 1])
+            if s == 2:
+                w4_q.append(deal_w4(1))
+            if s == PACK:
+                finish_block(0, lambda q, z_q: z_q0.append(z_q))
+        y = [psum.tile([P, BANK], F32, name="acc") for q in range(4)]
+        for q in range(4):
+            second_pass(0, y[q], z_q0[q])
+        fetch_draw(*slices[-1], h_prev)
+        fetch_push(*slices[-1], h_prev)
+
+        out_rows = out.rearrange("(n p) m -> p n m", p=P)
+
+        def finish_scores(q, z_q):
+            second_pass(1, y[q], z_q)
+            scores = ring.tile([P, BANK], F32, name="scores", bufs=4)
+            nc.scalar.activation(out=scores[:], in_=y[q][:], func=ACT.Sigmoid)
+            nc.sync.dma_start(
+                out=out_rows[:, :, QUARTER * q : QUARTER * (q + 1)],
+                in_=scores[:].rearrange("p (n c) -> p n c", c=QUARTER),
+            )
+
+        finish_block(1, finish_scores)

@@ -44,13 +44,11 @@ def tile_list_reed_voicing_scores_kernel(
         v_sc = held([P, 2 * S], U8, "v_sc")
         v_w = [held([P, S], U32, "v_w%d" % a) for a in range(2)]
         w4_sc_raw = held([P, 2, H], U8, "w4_sc_raw")
-        w8_sc = held([P, 2, N], U8, "w8_sc")
         gain_t = held([P, 2, PACK], F32, "gain_t")
 
         for a in range(2):
             nc.vector.memset(tab_sc[a][:].bitcast(I32), 0)
         nc.gpsimd.memset(w4_sc_raw[:].rearrange("p a c -> p (a c)").bitcast(I32), 0)
-        nc.vector.memset(w8_sc[:].rearrange("p a c -> p (a c)").bitcast(I32), 0)
         nc.vector.memset(v_sc[:].bitcast(I32), 0)
 
         def load_w1(b, a):
@@ -75,21 +73,16 @@ def tile_list_reed_voicing_scores_kernel(
         nc.sync.dma_start(pos2_t[:], pos2)
         for a in range(2):
             nc.sync.dma_start(out=tab_sc[a][0:P:8, :].bitcast(I32), in_=tab_scales[a].bitcast(I32))
-        load_tab(0)
-        w1_raw = {(0, a): load_w1(0, a) for a in range(2)}
+        for a in range(2):
+            load_tab(a)
         w4_raw = [load_w4(0)]
-        load_tab(1)
+        w1_raw = {(0, a): load_w1(0, a) for a in range(2)}
         for r in range(4):
             nc.gpsimd.dma_start(
                 out=w4_sc_raw[r:P:32].bitcast(I32),
                 in_=w4_scales[:, r:16:4, :].rearrange("a q c -> q a c").bitcast(I32),
             )
         nc.gpsimd.dma_start(out=gain_t[:], in_=gain.rearrange("(b p t) -> p b t", b=2, t=PACK))
-        for r in range(4):
-            nc.gpsimd.dma_start(
-                out=w8_sc[r:P:32].bitcast(I32),
-                in_=w8_scales[:, r:16:4, :].rearrange("a q c -> q a c").bitcast(I32),
-            )
 
         for a in range(2):
             nc.vector.tensor_copy(picked_sc[:, S * a : S * (a + 1)], tab_sc[a][:].indirect(offs_t[:]))
@@ -97,46 +90,55 @@ def tile_list_reed_voicing_scores_kernel(
             nc.sync.dma_start(out=v_sc[r:P:32, :].bitcast(I32), in_=picked_sc[8 * r : P : 32, :].bitcast(I32))
         nc.vector.tensor_copy(v_w[0][:], tab_w[0][:].indirect(offs_t[:]))
 
-        def round_w1(b, a):
+        def round_w1(b, a, copy):
             grouped = ring.tile([P, PACK * PASS], BF16, name="w1_bf", bufs=2, align_bytes=64)
-            nc.scalar.copy(
+            copy(
                 out=grouped[:].rearrange("p (t m j) -> p m j t", t=PACK, j=PACK),
                 in_=w1_raw[b, a][:].rearrange("p j (m t) -> p m j t", t=PACK),
             )
             return grouped
 
-        def quantize_w1(b, a, grouped):
+        def w1_planes(b, a):
             codes = held([P, PASS], U32, "w1_codes%d%d" % (b, a))
             scales = held([P, PASS], U8, "w1_scales%d%d" % (b, a))
-            nc.vector.quantize_mx(out=codes[:].bitcast(FP8X4), scales=scales[:], in_=grouped[:])
             return codes, scales
 
-        def deal_w4(b):
-            words = held([P, 2, PASS], U16, "w4_w%d" % b)
+        def quantize_w1(b, a, first, last):
+            codes, scales = w1_q[b, a]
+            nc.vector.quantize_mx(
+                out=codes[:, P * first : P * last].bitcast(FP8X4),
+                scales=scales[:, P * first : P * last],
+                in_=w1_bf[b, a][:, PASS * first : PASS * last],
+            )
+
+        def deal_w4_scales(b):
             scales = held([P, 2, PASS], U8, "w4_sc%d" % b)
-            nc.vector.tensor_copy(
+            nc.gpsimd.tensor_copy(
                 out=scales[:].rearrange("p a (t m) -> p a t m", t=PACK),
                 in_=w4_sc_raw[:, :, PASS * b : PASS * (b + 1)].rearrange("p a (m t) -> p a t m", t=PACK),
             )
-            nc.vector.tensor_copy(
+            return scales
+
+        def deal_w4_words(b):
+            words = held([P, 2, PASS], U16, "w4_w%d" % b)
+            nc.scalar.copy(
                 out=words[:].rearrange("p a (t m) -> p a t m", t=PACK),
                 in_=w4_raw[b][:].rearrange("p a (m t) -> p a t m", t=PACK),
             )
-            return words, scales
+            return words
 
-        def gather_words(half):
+        for half in range(2):
             nc.vector.tensor_copy(
                 v_w[1][:, BANK * half : BANK * (half + 1)],
                 tab_w[1][:].indirect(offs_t[:, 32 * half : 32 * (half + 1)]),
             )
-
-        w1_q = {}
-        w1_bf = {(0, a): round_w1(0, a) for a in range(2)}
-        w1_q[0, 0] = quantize_w1(0, 0, w1_bf[0, 0])
-        w4_q = [deal_w4(0)]
-        gather_words(0)
-        w1_q[0, 1] = quantize_w1(0, 1, w1_bf[0, 1])
-        gather_words(1)
+        w4_sc = [deal_w4_scales(b) for b in range(2)]
+        w4_w = [deal_w4_words(0)]
+        w1_q = {(b, a): w1_planes(b, a) for b in range(2) for a in range(2)}
+        w1_bf = {(0, 0): round_w1(0, 0, nc.scalar.copy), (0, 1): round_w1(0, 1, nc.vector.tensor_copy)}
+        for first, last in ((0, 1), (1, PACK)):
+            for a in range(2):
+                quantize_w1(0, a, first, last)
 
         for a in range(2):
             w1_raw[1, a] = load_w1(1, a)
@@ -145,6 +147,13 @@ def tile_list_reed_voicing_scores_kernel(
         nc.sync.dma_start(
             out=w8_w[:].bitcast(I32), in_=w8_words.rearrange("a p c i -> p a (c i)").bitcast(I32)
         )
+        w8_sc = held([P, 2, N], U8, "tab_w0")
+        nc.gpsimd.memset(w8_sc[:].rearrange("p a c -> p (a c)").bitcast(I32), 0)
+        for r in range(4):
+            nc.sync.dma_start(
+                out=w8_sc[r:P:32].bitcast(I32),
+                in_=w8_scales[:, r:16:4, :].rearrange("a q c -> q a c").bitcast(I32),
+            )
 
         def first_stage(b, t):
             rows = slice(P * t, P * (t + 1))
@@ -158,8 +167,8 @@ def tile_list_reed_voicing_scores_kernel(
                 for a in range(2):
                     nc.tensor.matmul_mx(
                         out=b_acc[:],
-                        lhsT=w4_q[b][0][:, a, rows].bitcast(FP4X4),
-                        lhsT_scale=w4_q[b][1][:, a, rows],
+                        lhsT=w4_w[b][:, a, rows].bitcast(FP4X4),
+                        lhsT_scale=w4_sc[b][:, a, rows],
                         rhs=v_w[a][:, cols].bitcast(FP8X4),
                         rhs_scale=v_sc[:, S * a + BANK * half : S * a + BANK * (half + 1)],
                         start=(a == 0),
@@ -183,7 +192,9 @@ def tile_list_reed_voicing_scores_kernel(
 
         def join(gb, prod):
             h = ring.tile([P, S], F32, name="h", bufs=3)
-            nc.vector.tensor_tensor(out=h[:], in0=prod[:], in1=gb[:], op=ALU.add)
+            for half in range(2):
+                cols = slice(BANK * half, BANK * (half + 1))
+                nc.gpsimd.tensor_tensor(out=h[:, cols], in0=prod[:, cols], in1=gb[:, cols], op=ALU.add)
             return h
 
         push = [held([P, PACK, PAIRS], F32, "push%d" % b) for b in range(2)]
@@ -246,10 +257,10 @@ def tile_list_reed_voicing_scores_kernel(
                 fetch_push(*slices[s - 1], h_prev)
             h_prev = h
             if s in (1, 2):
-                w1_bf[1, s - 1] = round_w1(1, s - 1)
-                w1_q[1, s - 1] = quantize_w1(1, s - 1, w1_bf[1, s - 1])
+                w1_bf[1, s - 1] = round_w1(1, s - 1, nc.scalar.copy)
+                quantize_w1(1, s - 1, 0, PACK)
             if s == 2:
-                w4_q.append(deal_w4(1))
+                w4_w.append(deal_w4_words(1))
             if s == PACK:
                 finish_block(0, lambda q, z_q: z_q0.append(z_q))
         y = [psum.tile([P, BANK], F32, name="acc") for q in range(4)]

@@ -38,17 +38,16 @@ def tile_list_reed_voicing_scores_kernel(
         offs_t = keep.tile([P, S // 16], U16, name="offs_t")
         pos1_t = keep.tile([P, PAIRS // 16], U16, name="pos1_t")
         pos2_t = keep.tile([P, PAIRS // 16], U16, name="pos2_t")
-        tab_sc = [held([P, T], U8, "tab_sc%d" % a) for a in range(2)]
+        tab_sc = held([P, T], U8, "tab_sc")
         tab_w = [held([P, T], U32, "tab_w%d" % a) for a in range(2)]
-        picked_sc = held([P, 2 * S], U8, "picked_sc")
+        picked_sc = held([P, S], U8, "picked_sc")
         v_sc = held([P, 2 * S], U8, "v_sc")
         v_w = [held([P, S], U32, "v_w%d" % a) for a in range(2)]
         w4_sc_raw = held([P, 2, H], U8, "w4_sc_raw")
         gain_t = held([P, 2, PACK], F32, "gain_t")
 
-        for a in range(2):
-            nc.vector.memset(tab_sc[a][:].bitcast(I32), 0)
-        nc.gpsimd.memset(w4_sc_raw[:].rearrange("p a c -> p (a c)").bitcast(I32), 0)
+        nc.vector.memset(tab_sc[:].bitcast(I32), 0)
+        nc.vector.memset(w4_sc_raw[:].rearrange("p a c -> p (a c)").bitcast(I32), 0)
         nc.vector.memset(v_sc[:].bitcast(I32), 0)
 
         def load_w1(b, a):
@@ -69,12 +68,12 @@ def tile_list_reed_voicing_scores_kernel(
             )
 
         nc.sync.dma_start(offs_t[:], offs)
+        for a in range(2):
+            nc.scalar.dma_start(out=tab_sc[a:P:8, :].bitcast(I32), in_=tab_scales[a].bitcast(I32))
+        load_tab(0)
         nc.sync.dma_start(pos1_t[:], pos1)
         nc.sync.dma_start(pos2_t[:], pos2)
-        for a in range(2):
-            nc.sync.dma_start(out=tab_sc[a][0:P:8, :].bitcast(I32), in_=tab_scales[a].bitcast(I32))
-        for a in range(2):
-            load_tab(a)
+        load_tab(1)
         w4_raw = [load_w4(0)]
         w1_raw = {(0, a): load_w1(0, a) for a in range(2)}
         for r in range(4):
@@ -84,10 +83,14 @@ def tile_list_reed_voicing_scores_kernel(
             )
         nc.gpsimd.dma_start(out=gain_t[:], in_=gain.rearrange("(b p t) -> p b t", b=2, t=PACK))
 
-        for a in range(2):
-            nc.vector.tensor_copy(picked_sc[:, S * a : S * (a + 1)], tab_sc[a][:].indirect(offs_t[:]))
+        nc.vector.tensor_copy(picked_sc[:], tab_sc[:].indirect(offs_t[:]))
         for r in range(4):
-            nc.sync.dma_start(out=v_sc[r:P:32, :].bitcast(I32), in_=picked_sc[8 * r : P : 32, :].bitcast(I32))
+            queue = nc.gpsimd if r == 3 else nc.sync
+            for a in range(2):
+                queue.dma_start(
+                    out=v_sc[r:P:32, S * a : S * (a + 1)].bitcast(I32),
+                    in_=picked_sc[8 * r + a : P : 32, :].bitcast(I32),
+                )
         nc.vector.tensor_copy(v_w[0][:], tab_w[0][:].indirect(offs_t[:]))
 
         def round_w1(b, a, copy):
@@ -159,7 +162,7 @@ def tile_list_reed_voicing_scores_kernel(
             rows = slice(P * t, P * (t + 1))
             g = gain_t[:, b, t : t + 1]
             gb = ring.tile([P, S], F32, name="gb", bufs=3)
-            prod = ring.tile([P, S], F32, name="prod", bufs=2)
+            prod = [ring.tile([P, BANK], F32, name="prod%d" % half, bufs=1) for half in range(2)]
             for half in range(2):
                 cols = slice(BANK * half, BANK * (half + 1))
                 b_acc = psum.tile([P, BANK], F32, name="acc")
@@ -186,15 +189,16 @@ def tile_list_reed_voicing_scores_kernel(
                     )
                 nc.scalar.activation(out=gb[:, cols], in_=b_acc[:], func=ACT.Copy, scale=g)
                 nc.vector.scalar_tensor_tensor(
-                    out=prod[:, cols], in0=gb[:, cols], scalar=g, in1=a_acc[:], op0=ALU.add, op1=ALU.mult
+                    out=prod[half][:], in0=gb[:, cols], scalar=g, in1=a_acc[:], op0=ALU.add, op1=ALU.mult
                 )
             return gb, prod
 
-        def join(gb, prod):
+        def join(gb, prod, first):
             h = ring.tile([P, S], F32, name="h", bufs=3)
+            engine = nc.vector if first else nc.gpsimd
             for half in range(2):
                 cols = slice(BANK * half, BANK * (half + 1))
-                nc.gpsimd.tensor_tensor(out=h[:, cols], in0=prod[:, cols], in1=gb[:, cols], op=ALU.add)
+                engine.tensor_tensor(out=h[:, cols], in0=prod[half][:], in1=gb[:, cols], op=ALU.add)
             return h
 
         push = [held([P, PACK, PAIRS], F32, "push%d" % b) for b in range(2)]
@@ -208,51 +212,46 @@ def tile_list_reed_voicing_scores_kernel(
         def fetch_push(b, t, h):
             nc.vector.tensor_copy(push[b][:, t, :], h[:].indirect(pos1_t[:]))
 
-        def make_z(b, q):
-            cols = slice(QUARTER * q, QUARTER * (q + 1))
-            z = ring.tile([P, PACK * QUARTER], BF16, name="z", bufs=4, align_bytes=64)
+        z = [held([P, PACK * PAIRS], BF16, "z%d" % b) for b in range(2)]
+        z_codes = [held([P, PAIRS], U32, "z_codes%d" % b) for b in range(2)]
+        z_scales = [held([P, PAIRS], U8, "z_scales%d" % b) for b in range(2)]
+
+        def make_z(b, first, last):
             nc.vector.tensor_tensor(
-                out=z[:].rearrange("p (c i t) -> p c t i", i=4, t=PACK),
-                in0=push[b][:, :, cols].rearrange("p t (c i) -> p c t i", i=4),
-                in1=size[b][:, :, cols].rearrange("p t (c i) -> p c t i", i=4),
+                out=z[b][:, PACK * first : PACK * last].rearrange("p (c i t) -> p c t i", i=4, t=PACK),
+                in0=push[b][:, :, first:last].rearrange("p t (c i) -> p c t i", i=4),
+                in1=size[b][:, :, first:last].rearrange("p t (c i) -> p c t i", i=4),
                 op=ALU.max,
             )
-            return z
 
-        def quantize_z(b, q, z):
-            codes = held([P, QUARTER], U32, "z_codes%d%d" % (b, q))
-            scales = held([P, QUARTER], U8, "z_scales%d%d" % (b, q))
-            nc.vector.quantize_mx(out=codes[:].bitcast(FP8X4), scales=scales[:], in_=z[:])
-            return codes, scales
+        def quantize_z(b, first, last):
+            nc.vector.quantize_mx(
+                out=z_codes[b][:, first:last].bitcast(FP8X4),
+                scales=z_scales[b][:, first:last],
+                in_=z[b][:, PACK * first : PACK * last],
+            )
 
-        def second_pass(b, y, z_q):
+        def second_pass(b, q):
+            pairs = slice(QUARTER * q, QUARTER * (q + 1))
             for n in range(4):
                 cols = slice(P * n, P * (n + 1))
                 nc.tensor.matmul_mx(
-                    out=y[:, cols],
+                    out=y[q][:, cols],
                     lhsT=w8_w[:, b, cols].bitcast(FP8X4),
                     lhsT_scale=w8_sc[:, b, cols],
-                    rhs=z_q[0][:].bitcast(FP8X4),
-                    rhs_scale=z_q[1][:],
+                    rhs=z_codes[b][:, pairs].bitcast(FP8X4),
+                    rhs_scale=z_scales[b][:, pairs],
                     start=(b == 0 and n == 0),
                     stop=(b == 1 and n == 3),
                 )
 
-        def finish_block(b, after):
-            z = [make_z(b, 0)]
-            for q in range(4):
-                if q < 3:
-                    z.append(make_z(b, q + 1))
-                after(q, quantize_z(b, q, z[q]))
-
         slices = [(b, t) for b in range(2) for t in range(PACK)]
-        z_q0 = []
         h_prev = None
         for s, (b, t) in enumerate(slices):
             gb, prod = first_stage(b, t)
             if s > 0:
                 fetch_draw(*slices[s - 1], h_prev)
-            h = join(gb, prod)
+            h = join(gb, prod, s == 0)
             if s > 0:
                 fetch_push(*slices[s - 1], h_prev)
             h_prev = h
@@ -262,17 +261,20 @@ def tile_list_reed_voicing_scores_kernel(
             if s == 2:
                 w4_w.append(deal_w4_words(1))
             if s == PACK:
-                finish_block(0, lambda q, z_q: z_q0.append(z_q))
+                make_z(0, 0, PAIRS)
+            if s == PACK + 1:
+                quantize_z(0, 0, PAIRS)
         y = [psum.tile([P, BANK], F32, name="acc") for q in range(4)]
         for q in range(4):
-            second_pass(0, y[q], z_q0[q])
+            second_pass(0, q)
         fetch_draw(*slices[-1], h_prev)
         fetch_push(*slices[-1], h_prev)
 
         out_rows = out.rearrange("(n p) m -> p n m", p=P)
 
-        def finish_scores(q, z_q):
-            second_pass(1, y[q], z_q)
+        def finish_scores(q):
+            quantize_z(1, QUARTER * q, QUARTER * (q + 1))
+            second_pass(1, q)
             scores = ring.tile([P, BANK], F32, name="scores", bufs=4)
             nc.scalar.activation(out=scores[:], in_=y[q][:], func=ACT.Sigmoid)
             nc.sync.dma_start(
@@ -280,4 +282,8 @@ def tile_list_reed_voicing_scores_kernel(
                 in_=scores[:].rearrange("p (n c) -> p n c", c=QUARTER),
             )
 
-        finish_block(1, finish_scores)
+        make_z(1, 0, QUARTER)
+        for q in range(4):
+            if q < 3:
+                make_z(1, QUARTER * (q + 1), QUARTER * (q + 2))
+            finish_scores(q)

@@ -30,7 +30,7 @@ def tile_list_reed_voicing_scores_kernel(
     with ExitStack() as ctx:
         keep = ctx.enter_context(tc.tile_pool(name="keep", bufs=1))
         ring = ctx.enter_context(tc.tile_pool(name="ring", bufs=2))
-        psum = ctx.enter_context(tc.psum_pool(name="psum", bufs=8))
+        psum = ctx.enter_context(tc.psum_pool(name="psum", bufs=1))
 
         def held(shape, dtype, name):
             return keep.tile(shape, dtype, name=name, align_bytes=64)
@@ -38,26 +38,30 @@ def tile_list_reed_voicing_scores_kernel(
         offs_t = keep.tile([P, S // 16], U16, name="offs_t")
         pos1_t = keep.tile([P, PAIRS // 16], U16, name="pos1_t")
         pos2_t = keep.tile([P, PAIRS // 16], U16, name="pos2_t")
-        tab_sc = held([P, T], U8, "tab_sc")
+        tab_sc = [held([P, T], U8, "tab_sc%d" % a) for a in range(2)]
         tab_w = [held([P, T], U32, "tab_w%d" % a) for a in range(2)]
-        picked_sc = held([P, S], U8, "picked_sc")
+        picked_sc = held([P, 2 * S], U8, "picked_sc")
         v_sc = held([P, 2 * S], U8, "v_sc")
         v_w = [held([P, S], U32, "v_w%d" % a) for a in range(2)]
         w4_sc_raw = held([P, 2, H], U8, "w4_sc_raw")
         gain_t = held([P, 2, PACK], F32, "gain_t")
 
-        nc.vector.memset(tab_sc[:].bitcast(I32), 0)
+        nc.gpsimd.memset(tab_sc[0][:].bitcast(I32), 0)
+        nc.vector.memset(tab_sc[1][:].bitcast(I32), 0)
         nc.vector.memset(w4_sc_raw[:].rearrange("p a c -> p (a c)").bitcast(I32), 0)
         nc.vector.memset(v_sc[:].bitcast(I32), 0)
 
-        def load_w1(b, a):
-            raw = ring.tile([P, PACK, PASS], F32, name="w1_raw", bufs=2)
-            rows = w1[PASS * a : PASS * (a + 1), PASS * b : PASS * (b + 1)]
-            nc.sync.dma_start(out=raw[:], in_=rows.rearrange("(p j) c -> p j c", j=PACK))
+        def load_w1(b, a, pieces):
+            raw = held([P, PACK, PASS], F32, "tab_sc1" if (b, a) == (0, 1) else "w1_raw%d%d" % (b, a))
+            rows = w1[PASS * a : PASS * (a + 1), PASS * b : PASS * (b + 1)].rearrange("(p j) c -> p j c", j=PACK)
+            width = PASS // pieces
+            for piece in range(pieces):
+                cols = slice(width * piece, width * (piece + 1))
+                nc.sync.dma_start(out=raw[:, :, cols], in_=rows[:, :, cols])
             return raw
 
         def load_w4(b):
-            raw = held([P, 2, PASS], U16, "w4_raw")
+            raw = held([P, 2, PASS], U16, "w4_raw%d" % b)
             cols = w4_words[:, :, 2 * PASS * b : 2 * PASS * (b + 1)]
             nc.sync.dma_start(out=raw[:].bitcast(I32), in_=cols.rearrange("a p c -> p a c").bitcast(I32))
             return raw
@@ -68,37 +72,37 @@ def tile_list_reed_voicing_scores_kernel(
             )
 
         nc.sync.dma_start(offs_t[:], offs)
-        for a in range(2):
-            nc.scalar.dma_start(out=tab_sc[a:P:8, :].bitcast(I32), in_=tab_scales[a].bitcast(I32))
-        load_tab(0)
         nc.sync.dma_start(pos1_t[:], pos1)
         nc.sync.dma_start(pos2_t[:], pos2)
-        load_tab(1)
-        w4_raw = [load_w4(0)]
-        w1_raw = {(0, a): load_w1(0, a) for a in range(2)}
+        for a in range(2):
+            nc.sync.dma_start(out=tab_sc[a][0:P:8, :].bitcast(I32), in_=tab_scales[a].bitcast(I32))
+        load_tab(0)
         for r in range(4):
-            nc.gpsimd.dma_start(
+            nc.sync.dma_start(
                 out=w4_sc_raw[r:P:32].bitcast(I32),
                 in_=w4_scales[:, r:16:4, :].rearrange("a q c -> q a c").bitcast(I32),
             )
+        load_tab(1)
+        w4_raw = [load_w4(0)]
+        w1_raw = {(0, 0): load_w1(0, 0, 1)}
         nc.gpsimd.dma_start(out=gain_t[:], in_=gain.rearrange("(b p t) -> p b t", b=2, t=PACK))
 
-        nc.vector.tensor_copy(picked_sc[:], tab_sc[:].indirect(offs_t[:]))
+        for a in range(2):
+            nc.vector.tensor_copy(picked_sc[:, S * a : S * (a + 1)], tab_sc[a][:].indirect(offs_t[:]))
         for r in range(4):
-            queue = nc.gpsimd if r == 3 else nc.sync
-            for a in range(2):
-                queue.dma_start(
-                    out=v_sc[r:P:32, S * a : S * (a + 1)].bitcast(I32),
-                    in_=picked_sc[8 * r + a : P : 32, :].bitcast(I32),
-                )
+            nc.sync.dma_start(out=v_sc[r:P:32, :].bitcast(I32), in_=picked_sc[8 * r : P : 32, :].bitcast(I32))
+        w1_raw[0, 1] = load_w1(0, 1, 2)
         nc.vector.tensor_copy(v_w[0][:], tab_w[0][:].indirect(offs_t[:]))
 
-        def round_w1(b, a, copy):
+        def round_w1(b, a, copy, pieces):
             grouped = ring.tile([P, PACK * PASS], BF16, name="w1_bf", bufs=2, align_bytes=64)
-            copy(
-                out=grouped[:].rearrange("p (t m j) -> p m j t", t=PACK, j=PACK),
-                in_=w1_raw[b, a][:].rearrange("p j (m t) -> p m j t", t=PACK),
-            )
+            count = P // pieces
+            for piece in range(pieces):
+                ms = slice(count * piece, count * (piece + 1))
+                copy(
+                    out=grouped[:].rearrange("p (t m j) -> p m j t", t=PACK, j=PACK)[:, ms],
+                    in_=w1_raw[b, a][:].rearrange("p j (m t) -> p m j t", t=PACK)[:, ms],
+                )
             return grouped
 
         def w1_planes(b, a):
@@ -114,13 +118,14 @@ def tile_list_reed_voicing_scores_kernel(
                 in_=w1_bf[b, a][:, PASS * first : PASS * last],
             )
 
-        def deal_w4_scales(b):
-            scales = held([P, 2, PASS], U8, "w4_sc%d" % b)
+        def deal_w4_scales(b, first, last, name):
+            scales = held([P, 2, last - first, P], U8, name)
+            block = w4_sc_raw[:, :, PASS * b : PASS * (b + 1)]
             nc.gpsimd.tensor_copy(
-                out=scales[:].rearrange("p a (t m) -> p a t m", t=PACK),
-                in_=w4_sc_raw[:, :, PASS * b : PASS * (b + 1)].rearrange("p a (m t) -> p a t m", t=PACK),
+                out=scales[:], in_=block.rearrange("p a (m t) -> p a t m", t=PACK)[:, :, first:last, :]
             )
-            return scales
+            for t in range(first, last):
+                w4_sc[b, t] = scales[:, :, t - first, :]
 
         def deal_w4_words(b):
             words = held([P, 2, PASS], U16, "w4_w%d" % b)
@@ -135,16 +140,19 @@ def tile_list_reed_voicing_scores_kernel(
                 v_w[1][:, BANK * half : BANK * (half + 1)],
                 tab_w[1][:].indirect(offs_t[:, 32 * half : 32 * (half + 1)]),
             )
-        w4_sc = [deal_w4_scales(b) for b in range(2)]
+        w4_sc = {}
+        deal_w4_scales(0, 0, 1, "w4_sc_first")
+        deal_w4_scales(1, 0, PACK, "w4_sc_last")
         w4_w = [deal_w4_words(0)]
         w1_q = {(b, a): w1_planes(b, a) for b in range(2) for a in range(2)}
-        w1_bf = {(0, 0): round_w1(0, 0, nc.scalar.copy), (0, 1): round_w1(0, 1, nc.vector.tensor_copy)}
+        w1_bf = {(0, 0): round_w1(0, 0, nc.scalar.copy, 1), (0, 1): round_w1(0, 1, nc.vector.tensor_copy, 2)}
         for first, last in ((0, 1), (1, PACK)):
             for a in range(2):
                 quantize_w1(0, a, first, last)
+        deal_w4_scales(0, 1, PACK, "tab_sc1")
 
         for a in range(2):
-            w1_raw[1, a] = load_w1(1, a)
+            w1_raw[1, a] = load_w1(1, a, 1)
         w4_raw.append(load_w4(1))
         w8_w = held([P, 2, N], U32, "tab_w1")
         nc.sync.dma_start(
@@ -162,16 +170,16 @@ def tile_list_reed_voicing_scores_kernel(
             rows = slice(P * t, P * (t + 1))
             g = gain_t[:, b, t : t + 1]
             gb = ring.tile([P, S], F32, name="gb", bufs=3)
-            prod = [ring.tile([P, BANK], F32, name="prod%d" % half, bufs=1) for half in range(2)]
+            prod = [ring.tile([P, BANK], F32, name="prod%d" % half, bufs=1, align_bytes=64) for half in range(2)]
             for half in range(2):
                 cols = slice(BANK * half, BANK * (half + 1))
-                b_acc = psum.tile([P, BANK], F32, name="acc")
-                a_acc = psum.tile([P, BANK], F32, name="acc")
+                b_acc = psum.tile([P, BANK], F32, name="b_acc", bufs=2)
+                a_acc = psum.tile([P, BANK], F32, name="a_acc", bufs=6)
                 for a in range(2):
                     nc.tensor.matmul_mx(
                         out=b_acc[:],
                         lhsT=w4_w[b][:, a, rows].bitcast(FP4X4),
-                        lhsT_scale=w4_sc[b][:, a, rows],
+                        lhsT_scale=w4_sc[b, t][:, a, :],
                         rhs=v_w[a][:, cols].bitcast(FP8X4),
                         rhs_scale=v_sc[:, S * a + BANK * half : S * a + BANK * (half + 1)],
                         start=(a == 0),
@@ -194,7 +202,7 @@ def tile_list_reed_voicing_scores_kernel(
             return gb, prod
 
         def join(gb, prod, first):
-            h = ring.tile([P, S], F32, name="h", bufs=3)
+            h = ring.tile([P, S], F32, name="h", bufs=3, align_bytes=64)
             engine = nc.vector if first else nc.gpsimd
             for half in range(2):
                 cols = slice(BANK * half, BANK * (half + 1))
@@ -204,16 +212,21 @@ def tile_list_reed_voicing_scores_kernel(
         push = [held([P, PACK, PAIRS], F32, "push%d" % b) for b in range(2)]
         size = [held([P, PACK, PAIRS], F32, "size%d" % b) for b in range(2)]
 
+        draws = {}
+
         def fetch_draw(b, t, h):
-            draw = ring.tile([P, PAIRS], F32, name="draw", bufs=2)
+            draw = ring.tile([P, PAIRS], F32, name="draw", bufs=4)
             nc.vector.tensor_copy(draw[:], h[:].indirect(pos2_t[:]))
-            nc.scalar.activation(out=size[b][:, t, :], in_=draw[:], func=ACT.Abs)
+            draws[b, t] = draw
+
+        def take_size(b, t):
+            nc.scalar.activation(out=size[b][:, t, :], in_=draws[b, t][:], func=ACT.Abs)
 
         def fetch_push(b, t, h):
             nc.vector.tensor_copy(push[b][:, t, :], h[:].indirect(pos1_t[:]))
 
         z = [held([P, PACK * PAIRS], BF16, "z%d" % b) for b in range(2)]
-        z_codes = [held([P, PAIRS], U32, "z_codes%d" % b) for b in range(2)]
+        z_codes = {1: held([P, PAIRS], U32, "z_codes")}
         z_scales = [held([P, PAIRS], U8, "z_scales%d" % b) for b in range(2)]
 
         def make_z(b, first, last):
@@ -256,19 +269,25 @@ def tile_list_reed_voicing_scores_kernel(
                 fetch_push(*slices[s - 1], h_prev)
             h_prev = h
             if s in (1, 2):
-                w1_bf[1, s - 1] = round_w1(1, s - 1, nc.scalar.copy)
+                w1_bf[1, s - 1] = round_w1(1, s - 1, nc.scalar.copy, 2)
                 quantize_w1(1, s - 1, 0, PACK)
             if s == 2:
                 w4_w.append(deal_w4_words(1))
             if s == PACK:
-                make_z(0, 0, PAIRS)
+                for early in slices[:PACK]:
+                    take_size(*early)
+            if s > PACK:
+                take_size(*slices[s - 1])
             if s == PACK + 1:
-                quantize_z(0, 0, PAIRS)
-        y = [psum.tile([P, BANK], F32, name="acc") for q in range(4)]
+                make_z(0, 0, PAIRS)
+        fetch_draw(*slices[-1], h_prev)
+        take_size(*slices[-1])
+        z_codes[0] = ring.tile([P, PAIRS], U32, name="prod1", bufs=1, align_bytes=64)
+        quantize_z(0, 0, PAIRS)
+        fetch_push(*slices[-1], h_prev)
+        y = [psum.tile([P, BANK], F32, name="a_acc", bufs=6) for q in range(4)]
         for q in range(4):
             second_pass(0, q)
-        fetch_draw(*slices[-1], h_prev)
-        fetch_push(*slices[-1], h_prev)
 
         out_rows = out.rearrange("(n p) m -> p n m", p=P)
 

from contextlib import ExitStack

import concourse.mybir as mybir

K, T, S, H, PAIRS, N = 1024, 2048, 1024, 1024, 512, 512
FLOPS = 2 * (2 * K * H * S + H * N * PAIRS)

F32 = mybir.dt.float32
BF16 = mybir.dt.bfloat16
I32 = mybir.dt.int32
U32 = mybir.dt.uint32
U16 = mybir.dt.uint16
U8 = mybir.dt.uint8
FP8X4 = mybir.dt.float8_e4m3fn_x4
FP4X4 = mybir.dt.float4_e2m1fn_x4
ALU = mybir.AluOpType
ACT = mybir.ActivationFunctionType

P = 128
PACK = 4
PASS = P * PACK
BANK = 512
QUARTER = 128


def tile_list_reed_voicing_scores_kernel(
    tc, tab_words, tab_scales, offs, w1, w4_words, w4_scales, gain, pos1, pos2, w8_words, w8_scales, out
):
    nc = tc.nc
    with ExitStack() as ctx:
        keep = ctx.enter_context(tc.tile_pool(name="keep", bufs=1))
        ring = ctx.enter_context(tc.tile_pool(name="ring", bufs=2))
        psum = ctx.enter_context(tc.psum_pool(name="psum", bufs=1))

        def held(shape, dtype, name):
            return keep.tile(shape, dtype, name=name, align_bytes=64)

        offs_t = keep.tile([P, S // 16], U16, name="offs_t")
        pos1_t = keep.tile([P, PAIRS // 16], U16, name="pos1_t")
        pos2_t = keep.tile([P, PAIRS // 16], U16, name="pos2_t")
        tab_sc = [held([P, T], U8, "tab_sc%d" % a) for a in range(2)]
        tab_w = [held([P, T], U32, "tab_w%d" % a) for a in range(2)]
        picked_sc = held([P, 2 * S], U8, "picked_sc")
        v_sc = held([P, 2 * S], U8, "v_sc")
        v_w = [held([P, S], U32, "v_w%d" % a) for a in range(2)]
        w4_sc_raw = held([P, 2, H], U8, "w4_sc_raw")
        gain_t = held([P, 2, PACK], F32, "gain_t")

        nc.gpsimd.memset(tab_sc[0][:].bitcast(I32), 0)
        nc.vector.memset(tab_sc[1][:].bitcast(I32), 0)
        nc.vector.memset(w4_sc_raw[:].rearrange("p a c -> p (a c)").bitcast(I32), 0)
        nc.vector.memset(v_sc[:].bitcast(I32), 0)

        def load_w1(b, a, pieces):
            raw = held([P, PACK, PASS], F32, "tab_sc1" if (b, a) == (0, 1) else "w1_raw%d%d" % (b, a))
            rows = w1[PASS * a : PASS * (a + 1), PASS * b : PASS * (b + 1)].rearrange("(p j) c -> p j c", j=PACK)
            width = PASS // pieces
            for piece in range(pieces):
                cols = slice(width * piece, width * (piece + 1))
                nc.sync.dma_start(out=raw[:, :, cols], in_=rows[:, :, cols])
            return raw

        def load_w4(b):
            raw = held([P, 2, PASS], U16, "w4_raw%d" % b)
            cols = w4_words[:, :, 2 * PASS * b : 2 * PASS * (b + 1)]
            nc.sync.dma_start(out=raw[:].bitcast(I32), in_=cols.rearrange("a p c -> p a c").bitcast(I32))
            return raw

        def load_tab(a):
            nc.sync.dma_start(
                out=tab_w[a][:].bitcast(I32), in_=tab_words[a].rearrange("p t i -> p (t i)").bitcast(I32)
            )

        nc.sync.dma_start(offs_t[:], offs)
        nc.sync.dma_start(pos1_t[:], pos1)
        nc.sync.dma_start(pos2_t[:], pos2)
        for a in range(2):
            nc.sync.dma_start(out=tab_sc[a][0:P:8, :].bitcast(I32), in_=tab_scales[a].bitcast(I32))
        load_tab(0)
        for r in range(4):
            nc.sync.dma_start(
                out=w4_sc_raw[r:P:32].bitcast(I32),
                in_=w4_scales[:, r:16:4, :].rearrange("a q c -> q a c").bitcast(I32),
            )
        load_tab(1)
        w4_raw = [load_w4(0)]
        w1_raw = {(0, 0): load_w1(0, 0, 1)}
        nc.gpsimd.dma_start(out=gain_t[:], in_=gain.rearrange("(b p t) -> p b t", b=2, t=PACK))

        for a in range(2):
            nc.vector.tensor_copy(picked_sc[:, S * a : S * (a + 1)], tab_sc[a][:].indirect(offs_t[:]))
        for r in range(4):
            nc.sync.dma_start(out=v_sc[r:P:32, :].bitcast(I32), in_=picked_sc[8 * r : P : 32, :].bitcast(I32))
        w1_raw[0, 1] = load_w1(0, 1, 2)
        nc.vector.tensor_copy(v_w[0][:], tab_w[0][:].indirect(offs_t[:]))

        def round_w1(b, a, copy, pieces):
            grouped = ring.tile([P, PACK * PASS], BF16, name="w1_bf", bufs=2, align_bytes=64)
            count = P // pieces
            for piece in range(pieces):
                ms = slice(count * piece, count * (piece + 1))
                copy(
                    out=grouped[:].rearrange("p (t m j) -> p m j t", t=PACK, j=PACK)[:, ms],
                    in_=w1_raw[b, a][:].rearrange("p j (m t) -> p m j t", t=PACK)[:, ms],
                )
            return grouped

        def w1_planes(b, a):
            codes = held([P, PASS], U32, "w1_codes%d%d" % (b, a))
            scales = held([P, PASS], U8, "w1_scales%d%d" % (b, a))
            return codes, scales

        def quantize_w1(b, a, first, last):
            codes, scales = w1_q[b, a]
            nc.vector.quantize_mx(
                out=codes[:, P * first : P * last].bitcast(FP8X4),
                scales=scales[:, P * first : P * last],
                in_=w1_bf[b, a][:, PASS * first : PASS * last],
            )

        def deal_w4_scales(b, first, last, name):
            scales = held([P, 2, last - first, P], U8, name)
            block = w4_sc_raw[:, :, PASS * b : PASS * (b + 1)]
            nc.gpsimd.tensor_copy(
                out=scales[:], in_=block.rearrange("p a (m t) -> p a t m", t=PACK)[:, :, first:last, :]
            )
            for t in range(first, last):
                w4_sc[b, t] = scales[:, :, t - first, :]

        def deal_w4_words(b):
            words = held([P, 2, PASS], U16, "w4_w%d" % b)
            nc.scalar.copy(
                out=words[:].rearrange("p a (t m) -> p a t m", t=PACK),
                in_=w4_raw[b][:].rearrange("p a (m t) -> p a t m", t=PACK),
            )
            return words

        for half in range(2):
            nc.vector.tensor_copy(
                v_w[1][:, BANK * half : BANK * (half + 1)],
                tab_w[1][:].indirect(offs_t[:, 32 * half : 32 * (half + 1)]),
            )
        w4_sc = {}
        deal_w4_scales(0, 0, 1, "w4_sc_first")
        deal_w4_scales(1, 0, PACK, "w4_sc_last")
        w4_w = [deal_w4_words(0)]
        w1_q = {(b, a): w1_planes(b, a) for b in range(2) for a in range(2)}
        w1_bf = {(0, 0): round_w1(0, 0, nc.scalar.copy, 1), (0, 1): round_w1(0, 1, nc.vector.tensor_copy, 2)}
        for first, last in ((0, 1), (1, PACK)):
            for a in range(2):
                quantize_w1(0, a, first, last)
        deal_w4_scales(0, 1, PACK, "tab_sc1")

        for a in range(2):
            w1_raw[1, a] = load_w1(1, a, 1)
        w4_raw.append(load_w4(1))
        w8_w = held([P, 2, N], U32, "tab_w1")
        nc.sync.dma_start(
            out=w8_w[:].bitcast(I32), in_=w8_words.rearrange("a p c i -> p a (c i)").bitcast(I32)
        )
        w8_sc = held([P, 2, N], U8, "tab_w0")
        nc.gpsimd.memset(w8_sc[:].rearrange("p a c -> p (a c)").bitcast(I32), 0)
        for r in range(4):
            nc.sync.dma_start(
                out=w8_sc[r:P:32].bitcast(I32),
                in_=w8_scales[:, r:16:4, :].rearrange("a q c -> q a c").bitcast(I32),
            )

        def first_stage(b, t):
            rows = slice(P * t, P * (t + 1))
            g = gain_t[:, b, t : t + 1]
            gb = ring.tile([P, S], F32, name="gb", bufs=3)
            prod = [ring.tile([P, BANK], F32, name="prod%d" % half, bufs=1, align_bytes=64) for half in range(2)]
            for half in range(2):
                cols = slice(BANK * half, BANK * (half + 1))
                b_acc = psum.tile([P, BANK], F32, name="b_acc", bufs=2)
                a_acc = psum.tile([P, BANK], F32, name="a_acc", bufs=6)
                for a in range(2):
                    nc.tensor.matmul_mx(
                        out=b_acc[:],
                        lhsT=w4_w[b][:, a, rows].bitcast(FP4X4),
                        lhsT_scale=w4_sc[b, t][:, a, :],
                        rhs=v_w[a][:, cols].bitcast(FP8X4),
                        rhs_scale=v_sc[:, S * a + BANK * half : S * a + BANK * (half + 1)],
                        start=(a == 0),
                        stop=(a == 1),
                    )
                for a in range(2):
                    nc.tensor.matmul_mx(
                        out=a_acc[:],
                        lhsT=w1_q[b, a][0][:, rows].bitcast(FP8X4),
                        lhsT_scale=w1_q[b, a][1][:, rows],
                        rhs=v_w[a][:, cols].bitcast(FP8X4),
                        rhs_scale=v_sc[:, S * a + BANK * half : S * a + BANK * (half + 1)],
                        start=(a == 0),
                        stop=(a == 1),
                    )
                nc.scalar.activation(out=gb[:, cols], in_=b_acc[:], func=ACT.Copy, scale=g)
                nc.vector.scalar_tensor_tensor(
                    out=prod[half][:], in0=gb[:, cols], scalar=g, in1=a_acc[:], op0=ALU.add, op1=ALU.mult
                )
            return gb, prod

        def join(gb, prod, first):
            h = ring.tile([P, S], F32, name="h", bufs=3, align_bytes=64)
            engine = nc.vector if first else nc.gpsimd
            for half in range(2):
                cols = slice(BANK * half, BANK * (half + 1))
                engine.tensor_tensor(out=h[:, cols], in0=prod[half][:], in1=gb[:, cols], op=ALU.add)
            return h

        push = [held([P, PACK, PAIRS], F32, "push%d" % b) for b in range(2)]
        size = [held([P, PACK, PAIRS], F32, "size%d" % b) for b in range(2)]

        draws = {}

        def fetch_draw(b, t, h):
            draw = ring.tile([P, PAIRS], F32, name="draw", bufs=4)
            nc.vector.tensor_copy(draw[:], h[:].indirect(pos2_t[:]))
            draws[b, t] = draw

        def take_size(b, t):
            nc.scalar.activation(out=size[b][:, t, :], in_=draws[b, t][:], func=ACT.Abs)

        def fetch_push(b, t, h):
            nc.vector.tensor_copy(push[b][:, t, :], h[:].indirect(pos1_t[:]))

        z = [held([P, PACK * PAIRS], BF16, "z%d" % b) for b in range(2)]
        z_codes = {1: held([P, PAIRS], U32, "z_codes")}
        z_scales = [held([P, PAIRS], U8, "z_scales%d" % b) for b in range(2)]

        def make_z(b, first, last):
            nc.vector.tensor_tensor(
                out=z[b][:, PACK * first : PACK * last].rearrange("p (c i t) -> p c t i", i=4, t=PACK),
                in0=push[b][:, :, first:last].rearrange("p t (c i) -> p c t i", i=4),
                in1=size[b][:, :, first:last].rearrange("p t (c i) -> p c t i", i=4),
                op=ALU.max,
            )

        def quantize_z(b, first, last):
            nc.vector.quantize_mx(
                out=z_codes[b][:, first:last].bitcast(FP8X4),
                scales=z_scales[b][:, first:last],
                in_=z[b][:, PACK * first : PACK * last],
            )

        def second_pass(b, q):
            pairs = slice(QUARTER * q, QUARTER * (q + 1))
            for n in range(4):
                cols = slice(P * n, P * (n + 1))
                nc.tensor.matmul_mx(
                    out=y[q][:, cols],
                    lhsT=w8_w[:, b, cols].bitcast(FP8X4),
                    lhsT_scale=w8_sc[:, b, cols],
                    rhs=z_codes[b][:, pairs].bitcast(FP8X4),
                    rhs_scale=z_scales[b][:, pairs],
                    start=(b == 0 and n == 0),
                    stop=(b == 1 and n == 3),
                )

        slices = [(b, t) for b in range(2) for t in range(PACK)]
        h_prev = None
        for s, (b, t) in enumerate(slices):
            gb, prod = first_stage(b, t)
            if s > 0:
                fetch_draw(*slices[s - 1], h_prev)
            h = join(gb, prod, s == 0)
            if s > 0:
                fetch_push(*slices[s - 1], h_prev)
            h_prev = h
            if s in (1, 2):
                w1_bf[1, s - 1] = round_w1(1, s - 1, nc.scalar.copy, 2)
                quantize_w1(1, s - 1, 0, PACK)
            if s == 2:
                w4_w.append(deal_w4_words(1))
            if s == PACK:
                for early in slices[:PACK]:
                    take_size(*early)
            if s > PACK:
                take_size(*slices[s - 1])
            if s == PACK + 1:
                make_z(0, 0, PAIRS)
        fetch_draw(*slices[-1], h_prev)
        take_size(*slices[-1])
        z_codes[0] = ring.tile([P, PAIRS], U32, name="prod1", bufs=1, align_bytes=64)
        quantize_z(0, 0, PAIRS)
        fetch_push(*slices[-1], h_prev)
        y = [psum.tile([P, BANK], F32, name="a_acc", bufs=6) for q in range(4)]
        for q in range(4):
            second_pass(0, q)

        out_rows = out.rearrange("(n p) m -> p n m", p=P)

        def finish_scores(q):
            quantize_z(1, QUARTER * q, QUARTER * (q + 1))
            second_pass(1, q)
            scores = ring.tile([P, BANK], F32, name="scores", bufs=4)
            nc.scalar.activation(out=scores[:], in_=y[q][:], func=ACT.Sigmoid)
            nc.sync.dma_start(
                out=out_rows[:, :, QUARTER * q : QUARTER * (q + 1)],
                in_=scores[:].rearrange("p (n c) -> p n c", c=QUARTER),
            )

        make_z(1, 0, QUARTER)
        for q in range(4):
            if q < 3:
                make_z(1, QUARTER * (q + 1), QUARTER * (q + 2))
            finish_scores(q)
